import numpy as np
import ml_dtypes


def mxq(x, axis, fmt="e4m3"):
    dtype, down = {"e4m3": (ml_dtypes.float8_e4m3fn, 7), "e5m2": (ml_dtypes.float8_e5m2, 14)}[fmt]
    v = np.moveaxis(np.asarray(x, np.float32).astype(ml_dtypes.bfloat16).astype(np.float64), axis, -1)
    blocks = v.reshape(v.shape[:-1] + (-1, 32))
    amax = np.abs(blocks).max(-1, keepdims=True)
    byte = np.maximum(np.where(amax > 0, np.frexp(amax)[1] - 1 + 127, 0) - down, 1)
    scale = np.exp2(byte - 127.0)
    codes = (blocks / scale).astype(np.float32).astype(dtype).astype(np.float64)
    return np.moveaxis((codes * scale).reshape(v.shape), -1, axis)


WIDE = False


def mx_kscale(k):
    if not WIDE:
        return np.ones(k)
    levels = np.array([10, -10, 5, -5, 0])
    if k % 512:
        return np.exp2(np.random.permutation(np.resize(levels, k // 32))).repeat(32)
    a = np.empty((k // 512, 16))
    for p in range(k // 512):
        a[p, :8] = np.random.permutation(np.resize(levels, 8))
        for g in range(8):
            far = levels[np.abs(levels - a[p, g]) >= 10]
            a[p, g + 8] = far[np.random.randint(len(far))]
    return np.exp2(a.ravel()).repeat(32)


def f64(x):
    return np.asarray(x).astype(np.float64)


def striped(idx):
    return np.tile(np.asarray(idx).reshape(-1, 16).T, (8, 1)).astype(np.uint16)


def unstriped(offs):
    return offs[:16].T.reshape(-1).astype(np.int64)


E2M1 = np.array([0.0, 0.5, 1.0, 1.5, 2.0, 3.0, 4.0, 6.0, -0.0, -0.5, -1.0, -1.5, -2.0, -3.0, -4.0, -6.0])


def pack_weight(w, fmt):
    k, n = w.shape
    w = f64(np.asarray(w, np.float32).astype(ml_dtypes.bfloat16)).reshape(k // 32, 32, n)
    amax = np.abs(w).max(1)
    if fmt == "e4m3":
        byte = np.frexp(amax)[1] - 1 + 127 - 7
    else:
        mant, ex = np.frexp(amax / 6.0)
        byte = np.where(mant > 0.5, ex, ex - 1) + 127
    byte = np.clip(np.where(amax > 0, byte, 1), 1, 254)
    scaled = (w * np.exp2(127.0 - byte)[:, None, :]).reshape(k, n).astype(np.float32)
    by_word = np.ascontiguousarray(scaled.reshape(k // 512, 128, 4, n).transpose(0, 1, 3, 2))
    if fmt == "e4m3":
        words = by_word.astype(ml_dtypes.float8_e4m3fn).view(np.uint8)
    else:
        c = by_word.astype(ml_dtypes.float4_e2m1fn).view(np.uint8) & 0xF
        words = (c[..., 0::2] | (c[..., 1::2] << 4)).reshape(k // 512, 128, 2 * n)
    return np.ascontiguousarray(words), np.ascontiguousarray(byte.astype(np.uint8).reshape(k // 512, 16, n))


def unpack_weight(words, scales, fmt):
    g, _, n = scales.shape
    words = np.ascontiguousarray(words).reshape(g, 128, n, -1)
    if fmt == "e4m3":
        vals = words.view(ml_dtypes.float8_e4m3fn).astype(np.float64)
    else:
        nib = np.empty((g, 128, n, 4), np.uint8)
        nib[..., 0::2] = words & 0xF
        nib[..., 1::2] = words >> 4
        vals = E2M1[nib]
    vals = vals * np.repeat(np.exp2(scales.astype(np.float64) - 127.0), 8, axis=1)[..., None]
    return vals.transpose(0, 1, 3, 2).reshape(g * 512, n)


D, E, T, I, Q, G = 512, 512, 2048, 512, 512, 64


def setup_inputs():
    n = np.random.standard_normal
    idx = np.random.permutation(T)[:I]
    fd = mx_kscale(D)
    fe = mx_kscale(E)
    keysp = pack_weight(n((D, T)) / fd[:, None], "e4m3")
    valsp = pack_weight(n((E, T)) / fe[:, None], "e4m3")
    return {
        "query": (n((D, Q)) * 0.5 / np.sqrt(D) * fd[:, None]).astype(np.float32),
        "keys_words": keysp[0],
        "keys_scales": keysp[1],
        "sharp": (np.random.uniform(0.5, 2.0, (I, 1))).astype(np.float32),
        "lse": (np.random.uniform(6.2, 6.5, (1, Q))).astype(np.float32),
        "gout": (n((E, Q)) * 1 / np.sqrt(E) * fe[:, None]).astype(np.float32),
        "vals_words": valsp[0],
        "vals_scales": valsp[1],
        "delta": (np.random.uniform(-0.3, 0.3, (1, Q))).astype(np.float32),
        "old": (1.0 * n((I, G))).astype(np.float32),
        "offs": striped(idx),
    }


def reference(query, keys_words, keys_scales, sharp, lse, gout, vals_words, vals_scales, delta, old, offs):
    idx = unstriped(offs)
    keysu = unpack_weight(keys_words, keys_scales, "e4m3")
    valsu = unpack_weight(vals_words, vals_scales, "e4m3")
    keysidxg = keysu[:, idx]
    queryq = mxq(f64(query), 0, "e4m3")
    a = keysidxg.T @ queryq
    valsidxg = valsu[:, idx]
    goutq = mxq(f64(gout), 0, "e4m3")
    dp = valsidxg.T @ goutq
    ds = np.exp(a * f64(sharp) - f64(lse)) * (dp - f64(delta)) * a * 512.0
    y = ds.reshape(I, G, Q // G).sum(axis=2) + f64(old)
    return y

@@ -1,0 +1,204 @@
+from contextlib import ExitStack
+
+import concourse.mybir as mybir
+
+D, E, T, I, Q, G = 512, 512, 2048, 512, 512, 64
+FLOPS = 2 * I * Q * (D + E)
+
+F32 = mybir.dt.float32
+BF16 = mybir.dt.bfloat16
+I32 = mybir.dt.int32
+U32 = mybir.dt.uint32
+U16 = mybir.dt.uint16
+U8 = mybir.dt.uint8
+FP8X4 = mybir.dt.float8_e4m3fn_x4
+ALU = mybir.AluOpType
+ACT = mybir.ActivationFunctionType
+
+P = 128
+PACK = 4
+TILES = Q // P
+BLOCKS = I // P
+HALF = Q // 2
+VAL_ROW = 4
+KEY_POOL_AT = 0
+KEY_SCALE_AT = KEY_POOL_AT
+VAL_POOL_AT = KEY_SCALE_AT + I
+KEY_BYTES_AT = VAL_POOL_AT + 4 * T
+GOUT_AT = KEY_BYTES_AT
+QUERY_AT = GOUT_AT + 4 * PACK * Q
+OLD_AT = QUERY_AT
+SHARP_AT = QUERY_AT + 4 * PACK * Q
+LSE_AT = SHARP_AT + 32
+VAL_BYTES_AT = LSE_AT + 32
+DELTA_AT = VAL_BYTES_AT
+WORDS_AT = VAL_BYTES_AT + T
+ZEROS_AT = SHARP_AT - 32
+ZEROS_WORDS = (WORDS_AT + 32 - ZEROS_AT) // 4
+
+
+def tile_attend_gsharpness_kernel(
+    tc, query, keys_words, keys_scales, sharp, lse, gout, vals_words, vals_scales, delta, old, offs, out
+):
+    nc = tc.nc
+    with ExitStack() as ctx:
+        held = ctx.enter_context(tc.tile_pool(name="held", bufs=1))
+        staged = ctx.enter_context(tc.tile_pool(name="staged", bufs=1))
+        psum = ctx.enter_context(tc.psum_pool(name="psum", bufs=1))
+
+        offsets = held.tile([P, I // 16], U16, name="offsets")
+        nc.sync.dma_start(offsets[:], offs)
+
+        def bank(n):
+            return psum.tile([P, BLOCKS * P], F32, name="bank%d" % n, tag="bank%d" % n)
+
+        def load_scales(pool_bytes, scales, row):
+            for quad in range(4):
+                nc.sync.dma_start(
+                    pool_bytes[32 * quad + row : 32 * quad + row + 4, :].bitcast(I32),
+                    scales[0, 4 * quad : 4 * quad + 4, :].bitcast(I32),
+                )
+
+        def words_in_hbm(words):
+            return words[0].rearrange("p t r -> p (t r)").bitcast(I32)
+
+        def load_rows(raw, rows):
+            for half in range(2):
+                nc.sync.dma_start(
+                    raw[:, half, :, :], rows.rearrange("(p t) c -> p t c", t=PACK)[:, :, half * HALF : (half + 1) * HALF]
+                )
+
+        key_pool = staged.tile([P, T], I32, name="key_pool", offset=KEY_POOL_AT)
+        nc.sync.dma_start(key_pool[:], words_in_hbm(keys_words))
+
+        key_bytes = staged.tile([P, T], U8, name="key_bytes", offset=KEY_BYTES_AT)
+        nc.gpsimd.memset(key_bytes[:].bitcast(I32), 0)
+        load_scales(key_bytes, keys_scales, 0)
+
+        zeros = staged.tile([P, ZEROS_WORDS], F32, name="zeros", offset=ZEROS_AT)
+        nc.gpsimd.memset(zeros[:, :P], 0.0)
+        identity = held.tile([P, P], F32, name="identity")
+        nc.gpsimd.affine_select(
+            out=identity[:], in_=zeros[:, :P], compare_op=ALU.not_equal, fill=1.0, base=0, pattern=[[-1, P]], channel_multiplier=1
+        )
+        sharp_col = staged.tile([P, BLOCKS], F32, name="sharp_col", offset=SHARP_AT)
+        nc.sync.dma_start(sharp_col[:], sharp.rearrange("(p b) o -> p (b o)", b=BLOCKS))
+        lse_col = staged.tile([P, TILES], F32, name="lse_col", offset=LSE_AT)
+        nc.sync.dma_start(lse_col[:], lse.rearrange("o (m j) -> m (o j)", j=TILES))
+        query_raw = staged.tile([P, 2, PACK, HALF], F32, name="query_raw", offset=QUERY_AT)
+        load_rows(query_raw, query)
+
+        val_bytes = staged.tile([P, T], U8, name="val_bytes", offset=VAL_BYTES_AT)
+        nc.vector.memset(val_bytes[:].bitcast(I32), 0)
+        load_scales(val_bytes, vals_scales, VAL_ROW)
+
+        warm = held.tile([P, 1], F32, name="warm")
+        nc.scalar.activation(warm[:], identity[:, 0:1], ACT.Exp)
+
+        neg_lse = held.tile([P, TILES], F32, name="neg_lse")
+        nc.scalar.mul(neg_lse[:], lse_col[:], -1.0)
+
+        sharp_bank = bank(4)
+        for b in range(BLOCKS):
+            nc.tensor.transpose(
+                sharp_bank[:, b * P : (b + 1) * P], sharp_col[:, b : b + 1].to_broadcast([P, P]), identity[:]
+            )
+        sharp_row = held.tile([P, I], F32, name="sharp_row")
+        nc.scalar.copy(sharp_row[:], sharp_bank[:])
+
+        def gather(picked, window):
+            nc.vector.tensor_copy(picked[:], window.indirect(offsets[:]))
+
+        def round_and_deal(copy, dealt, raw, half, m0, m1):
+            base = half * (P // 2)
+            copy(
+                dealt[:, :, base + m0 : base + m1, :].rearrange("p j m t -> p m t j"),
+                raw[:, half, :, m0 * TILES : m1 * TILES].rearrange("p t (m j) -> p m t j", j=TILES),
+            )
+
+        def quantise(name, dealt):
+            codes = held.tile([P, Q], U32, name=name + "_codes", align_bytes=64)
+            scales = held.tile([P, Q], U8, name=name + "_scales", align_bytes=64)
+            for pair in range(2):
+                cols = slice(pair * 2 * P, (pair + 1) * 2 * P)
+                nc.vector.quantize_mx(
+                    codes[:, cols].bitcast(FP8X4),
+                    scales[:, cols],
+                    dealt[:, 2 * pair : 2 * pair + 2, :, :].rearrange("p j m t -> p (j m t)"),
+                )
+            return codes, scales
+
+        def product(acc, codes, scales, j, words, word_scales):
+            cols = slice(j * P, (j + 1) * P)
+            nc.tensor.matmul_mx(
+                acc[:], lhsT=codes[:, cols].bitcast(FP8X4), lhsT_scale=scales[:, cols],
+                rhs=words[:].bitcast(FP8X4), rhs_scale=word_scales, start=True, stop=True,
+            )
+
+        def by_block(acc):
+            return acc[:].rearrange("m (p b) -> m b p", b=BLOCKS)
+
+        def blocks(tile):
+            return tile[:].rearrange("m (b p) -> m b p", b=BLOCKS)
+
+        key_words = staged.tile([P, I], U32, name="key_words", offset=WORDS_AT, align_bytes=64)
+        gather(key_words, key_pool[:].bitcast(U32))
+        val_pool = staged.tile([P, T], I32, name="val_pool", offset=VAL_POOL_AT)
+        nc.sync.dma_start(val_pool[:], words_in_hbm(vals_words))
+        key_scale = staged.tile([P, I], U8, name="key_scale", offset=KEY_SCALE_AT, align_bytes=64)
+        gather(key_scale, key_bytes[:])
+        gout_raw = staged.tile([P, 2, PACK, HALF], F32, name="gout_raw", offset=GOUT_AT)
+        load_rows(gout_raw, gout)
+
+        query_dealt = held.tile([P, TILES, P, PACK], BF16, name="query_dealt", tag="query_dealt", align_bytes=64)
+        round_and_deal(nc.scalar.copy, query_dealt, query_raw, 0, 0, 64)
+        round_and_deal(nc.scalar.copy, query_dealt, query_raw, 1, 0, 24)
+        round_and_deal(nc.vector.tensor_copy, query_dealt, query_raw, 1, 24, 64)
+        query_codes, query_scales = quantise("query", query_dealt)
+        val_scale = held.tile([P, I], U8, name="val_scale", tag="query_dealt", align_bytes=64)
+        gather(val_scale, val_bytes[:])
+        delta_col = staged.tile([P, TILES], F32, name="delta_col", offset=DELTA_AT)
+        nc.sync.dma_start(delta_col[:], delta.rearrange("o (m j) -> m (o j)", j=TILES))
+        old_rows = staged.tile([P, BLOCKS * G], F32, name="old_rows", offset=OLD_AT)
+        nc.sync.dma_start(old_rows[:], old.rearrange("(p b) g -> p (b g)", b=BLOCKS))
+
+        scores = [bank(j) for j in range(TILES)]
+        weighted = []
+        exps = []
+        for j in range(TILES):
+            product(scores[j], query_codes, query_scales, j, key_words, key_scale[:])
+            logits = held.tile([P, I], F32, name="logits%d" % j, tag="logits%d" % j, align_bytes=64)
+            nc.vector.tensor_tensor(blocks(logits), by_block(scores[j]), blocks(sharp_row), ALU.mult)
+            weights = held.tile([P, I], F32, name="weights%d" % j)
+            nc.scalar.activation(weights[:], logits[:], ACT.Exp, bias=neg_lse[:, j : j + 1], scale=1.0)
+            exps.append(weights)
+        val_words = staged.tile([P, I], U32, name="val_words2", offset=WORDS_AT, align_bytes=64)
+        gather(val_words, val_pool[:].bitcast(U32))
+        for j in range(TILES):
+            both = held.tile([P, I], F32, name="weighted%d" % j)
+            nc.vector.scalar_tensor_tensor(blocks(both), by_block(scores[j]), 512.0, blocks(exps[j]), ALU.mult, ALU.mult)
+            weighted.append(both)
+
+        gout_dealt = held.tile([P, TILES, P, PACK], BF16, name="gout_dealt", tag="logits%d" % (TILES - 1), align_bytes=64)
+        round_and_deal(nc.scalar.copy, gout_dealt, gout_raw, 0, 0, 64)
+        round_and_deal(nc.scalar.copy, gout_dealt, gout_raw, 1, 0, 64)
+        gout_codes, gout_scales = quantise("gout", gout_dealt)
+
+        sums = bank(0)
+        for j in range(TILES):
+            grad_bank = bank(4 + j)
+            product(grad_bank, gout_codes, gout_scales, j, val_words, val_scale[VAL_ROW:, :])
+            terms = held.tile([P, I], F32, name="terms%d" % j)
+            nc.vector.scalar_tensor_tensor(
+                blocks(terms), by_block(grad_bank), delta_col[:, j : j + 1], blocks(weighted[j]), ALU.subtract, ALU.mult
+            )
+            for b in range(BLOCKS):
+                nc.tensor.matmul(
+                    sums[:, b * P : (b + 1) * P], lhsT=terms[:, b * P : (b + 1) * P], rhs=identity[:],
+                    is_transpose=True, start=(j == 0 and b == 0), stop=(j == TILES - 1 and b == BLOCKS - 1),
+                )
+        pair_sums = held.tile([P, BLOCKS * G], F32, name="pair_sums")
+        nc.vector.tensor_reduce(pair_sums[:], sums[:].rearrange("p (c r) -> p c r", r=2), mybir.AxisListType.X, ALU.add)
+        result = held.tile([P, BLOCKS * G], F32, name="result")
+        nc.vector.tensor_tensor(result[:], pair_sums[:], old_rows[:], ALU.add)
+        nc.sync.dma_start(out.rearrange("(p b) g -> p (b g)", b=BLOCKS), result[:])

@@ -21,20 +21,19 @@ TILES = Q // P
 BLOCKS = I // P
 HALF = Q // 2
 VAL_ROW = 4
-KEY_POOL_AT = 0
-KEY_SCALE_AT = KEY_POOL_AT
-VAL_POOL_AT = KEY_SCALE_AT + I
-KEY_BYTES_AT = VAL_POOL_AT + 4 * T
-GOUT_AT = KEY_BYTES_AT
-QUERY_AT = GOUT_AT + 4 * PACK * Q
-OLD_AT = QUERY_AT
-SHARP_AT = QUERY_AT + 4 * PACK * Q
-LSE_AT = SHARP_AT + 32
-VAL_BYTES_AT = LSE_AT + 32
-DELTA_AT = VAL_BYTES_AT
-WORDS_AT = VAL_BYTES_AT + T
-ZEROS_AT = SHARP_AT - 32
+QUERY_AT = 0
+VAL_BYTES_AT = QUERY_AT + 4 * PACK * Q
+MINUS_AT = VAL_BYTES_AT + T
+KEY_SCALE_AT = MINUS_AT + 64
+WORDS_AT = KEY_SCALE_AT + I
+ZEROS_AT = VAL_BYTES_AT - 32
 ZEROS_WORDS = (WORDS_AT + 32 - ZEROS_AT) // 4
+VAL_POOL_AT = WORDS_AT + 4 * I
+DELTA_AT = VAL_POOL_AT + 4 * T
+OLD_AT = DELTA_AT + 32
+GOUT_AT = OLD_AT + 4 * BLOCKS * G
+LSE_AT = DELTA_AT - 32
+LSE_WORDS = (GOUT_AT + 32 - LSE_AT) // 4
 
 
 def tile_attend_gsharpness_kernel(
@@ -68,10 +67,14 @@ def tile_attend_gsharpness_kernel(
                     raw[:, half, :, :], rows.rearrange("(p t) c -> p t c", t=PACK)[:, :, half * HALF : (half + 1) * HALF]
                 )
 
-        key_pool = staged.tile([P, T], I32, name="key_pool", offset=KEY_POOL_AT)
+        lse_col = staged.tile([P, LSE_WORDS], F32, name="lse_col", offset=LSE_AT)
+        nc.sync.dma_start(lse_col[:, :TILES], lse.rearrange("o (m j) -> m (o j)", j=TILES))
+        sharp_col = held.tile([P, BLOCKS], F32, name="sharp_col")
+        nc.sync.dma_start(sharp_col[:], sharp.rearrange("(p b) o -> p (b o)", b=BLOCKS))
+        key_pool = held.tile([P, T], I32, name="key_pool")
         nc.sync.dma_start(key_pool[:], words_in_hbm(keys_words))
 
-        key_bytes = staged.tile([P, T], U8, name="key_bytes", offset=KEY_BYTES_AT)
+        key_bytes = held.tile([P, T], U8, name="key_bytes")
         nc.gpsimd.memset(key_bytes[:].bitcast(I32), 0)
         load_scales(key_bytes, keys_scales, 0)
 
@@ -81,10 +84,6 @@ def tile_attend_gsharpness_kernel(
         nc.gpsimd.affine_select(
             out=identity[:], in_=zeros[:, :P], compare_op=ALU.not_equal, fill=1.0, base=0, pattern=[[-1, P]], channel_multiplier=1
         )
-        sharp_col = staged.tile([P, BLOCKS], F32, name="sharp_col", offset=SHARP_AT)
-        nc.sync.dma_start(sharp_col[:], sharp.rearrange("(p b) o -> p (b o)", b=BLOCKS))
-        lse_col = staged.tile([P, TILES], F32, name="lse_col", offset=LSE_AT)
-        nc.sync.dma_start(lse_col[:], lse.rearrange("o (m j) -> m (o j)", j=TILES))
         query_raw = staged.tile([P, 2, PACK, HALF], F32, name="query_raw", offset=QUERY_AT)
         load_rows(query_raw, query)
 
@@ -92,18 +91,26 @@ def tile_attend_gsharpness_kernel(
         nc.vector.memset(val_bytes[:].bitcast(I32), 0)
         load_scales(val_bytes, vals_scales, VAL_ROW)
 
-        warm = held.tile([P, 1], F32, name="warm")
-        nc.scalar.activation(warm[:], identity[:, 0:1], ACT.Exp)
-
+        minus_one = staged.tile([P, 1], F32, name="minus_one", offset=MINUS_AT)
+        nc.vector.memset(minus_one[:], -1.0)
         neg_lse = held.tile([P, TILES], F32, name="neg_lse")
-        nc.scalar.mul(neg_lse[:], lse_col[:], -1.0)
+        nc.scalar.activation(neg_lse[:], lse_col[:, :TILES], ACT.Copy, scale=minus_one[:])
+
+        gout_raw = staged.tile([P, 2, PACK, HALF], F32, name="gout_raw", offset=GOUT_AT)
+        load_rows(gout_raw, gout)
+        val_pool = staged.tile([P, T], I32, name="val_pool", offset=VAL_POOL_AT)
+        nc.sync.dma_start(val_pool[:], words_in_hbm(vals_words))
+        delta_col = staged.tile([P, TILES], F32, name="delta_col", offset=DELTA_AT)
+        nc.sync.dma_start(delta_col[:], delta.rearrange("o (m j) -> m (o j)", j=TILES))
+        old_rows = staged.tile([P, BLOCKS * G], F32, name="old_rows", offset=OLD_AT)
+        nc.sync.dma_start(old_rows[:], old.rearrange("(p b) g -> p (b g)", b=BLOCKS))
 
         sharp_bank = bank(4)
         for b in range(BLOCKS):
             nc.tensor.transpose(
                 sharp_bank[:, b * P : (b + 1) * P], sharp_col[:, b : b + 1].to_broadcast([P, P]), identity[:]
             )
-        sharp_row = held.tile([P, I], F32, name="sharp_row")
+        sharp_row = held.tile([P, I], F32, name="sharp_row", tag="sharp_row", align_bytes=64)
         nc.scalar.copy(sharp_row[:], sharp_bank[:])
 
         def gather(picked, window):
@@ -116,22 +123,12 @@ def tile_attend_gsharpness_kernel(
                 raw[:, half, :, m0 * TILES : m1 * TILES].rearrange("p t (m j) -> p m t j", j=TILES),
             )
 
-        def quantise(name, dealt):
-            codes = held.tile([P, Q], U32, name=name + "_codes", align_bytes=64)
-            scales = held.tile([P, Q], U8, name=name + "_scales", align_bytes=64)
-            for pair in range(2):
-                cols = slice(pair * 2 * P, (pair + 1) * 2 * P)
-                nc.vector.quantize_mx(
-                    codes[:, cols].bitcast(FP8X4),
-                    scales[:, cols],
-                    dealt[:, 2 * pair : 2 * pair + 2, :, :].rearrange("p j m t -> p (j m t)"),
-                )
-            return codes, scales
+        def quantise(codes, scales, dealt):
+            nc.vector.quantize_mx(codes.bitcast(FP8X4), scales, dealt.rearrange("p j m t -> p (j m t)"))
 
-        def product(acc, codes, scales, j, words, word_scales):
-            cols = slice(j * P, (j + 1) * P)
+        def product(acc, codes, scales, words, word_scales):
             nc.tensor.matmul_mx(
-                acc[:], lhsT=codes[:, cols].bitcast(FP8X4), lhsT_scale=scales[:, cols],
+                acc[:], lhsT=codes.bitcast(FP8X4), lhsT_scale=scales,
                 rhs=words[:].bitcast(FP8X4), rhs_scale=word_scales, start=True, stop=True,
             )
 
@@ -143,62 +140,66 @@ def tile_attend_gsharpness_kernel(
 
         key_words = staged.tile([P, I], U32, name="key_words", offset=WORDS_AT, align_bytes=64)
         gather(key_words, key_pool[:].bitcast(U32))
-        val_pool = staged.tile([P, T], I32, name="val_pool", offset=VAL_POOL_AT)
-        nc.sync.dma_start(val_pool[:], words_in_hbm(vals_words))
         key_scale = staged.tile([P, I], U8, name="key_scale", offset=KEY_SCALE_AT, align_bytes=64)
         gather(key_scale, key_bytes[:])
-        gout_raw = staged.tile([P, 2, PACK, HALF], F32, name="gout_raw", offset=GOUT_AT)
-        load_rows(gout_raw, gout)
 
         query_dealt = held.tile([P, TILES, P, PACK], BF16, name="query_dealt", tag="query_dealt", align_bytes=64)
         round_and_deal(nc.scalar.copy, query_dealt, query_raw, 0, 0, 64)
-        round_and_deal(nc.scalar.copy, query_dealt, query_raw, 1, 0, 24)
-        round_and_deal(nc.vector.tensor_copy, query_dealt, query_raw, 1, 24, 64)
-        query_codes, query_scales = quantise("query", query_dealt)
+        round_and_deal(nc.scalar.copy, query_dealt, query_raw, 1, 0, 18)
+        round_and_deal(nc.vector.tensor_copy, query_dealt, query_raw, 1, 18, 64)
+        query_codes = [held.tile([P, P], U32, name="query_codes%d" % j, align_bytes=64) for j in range(TILES)]
+        query_scales = [held.tile([P, P], U8, name="query_scales%d" % j, align_bytes=64) for j in range(TILES)]
+        for j in range(TILES):
+            quantise(query_codes[j][:], query_scales[j][:], query_dealt[:, j : j + 1, :, :])
+        gout_dealt = held.tile([P, TILES, P, PACK], BF16, name="gout_dealt", align_bytes=64)
+        round_and_deal(nc.scalar.copy, gout_dealt, gout_raw, 0, 0, 64)
+        round_and_deal(nc.scalar.copy, gout_dealt, gout_raw, 1, 0, 64)
         val_scale = held.tile([P, I], U8, name="val_scale", tag="query_dealt", align_bytes=64)
         gather(val_scale, val_bytes[:])
-        delta_col = staged.tile([P, TILES], F32, name="delta_col", offset=DELTA_AT)
-        nc.sync.dma_start(delta_col[:], delta.rearrange("o (m j) -> m (o j)", j=TILES))
-        old_rows = staged.tile([P, BLOCKS * G], F32, name="old_rows", offset=OLD_AT)
-        nc.sync.dma_start(old_rows[:], old.rearrange("(p b) g -> p (b g)", b=BLOCKS))
 
         scores = [bank(j) for j in range(TILES)]
         weighted = []
         exps = []
         for j in range(TILES):
-            product(scores[j], query_codes, query_scales, j, key_words, key_scale[:])
-            logits = held.tile([P, I], F32, name="logits%d" % j, tag="logits%d" % j, align_bytes=64)
+            product(scores[j], query_codes[j][:], query_scales[j][:], key_words, key_scale[:])
+            logits = held.tile([P, I], F32, name="logits%d" % j)
             nc.vector.tensor_tensor(blocks(logits), by_block(scores[j]), blocks(sharp_row), ALU.mult)
-            weights = held.tile([P, I], F32, name="weights%d" % j)
+            weights = staged.tile([P, I], F32, name="weights%d" % j, offset=GOUT_AT + 4 * I * j)
             nc.scalar.activation(weights[:], logits[:], ACT.Exp, bias=neg_lse[:, j : j + 1], scale=1.0)
             exps.append(weights)
+        gout_codes = held.tile([P, Q], U32, name="gout_codes", tag="sharp_row", align_bytes=64)
+        gout_scales = held.tile([P, Q], U8, name="gout_scales", align_bytes=64)
+        quantise(gout_codes[:], gout_scales[:], gout_dealt[:])
         val_words = staged.tile([P, I], U32, name="val_words2", offset=WORDS_AT, align_bytes=64)
         gather(val_words, val_pool[:].bitcast(U32))
         for j in range(TILES):
-            both = held.tile([P, I], F32, name="weighted%d" % j)
+            both = staged.tile([P, I], F32, name="weighted%d" % j, offset=VAL_POOL_AT + 4 * I * j)
             nc.vector.scalar_tensor_tensor(blocks(both), by_block(scores[j]), 512.0, blocks(exps[j]), ALU.mult, ALU.mult)
             weighted.append(both)
 
-        gout_dealt = held.tile([P, TILES, P, PACK], BF16, name="gout_dealt", tag="logits%d" % (TILES - 1), align_bytes=64)
-        round_and_deal(nc.scalar.copy, gout_dealt, gout_raw, 0, 0, 64)
-        round_and_deal(nc.scalar.copy, gout_dealt, gout_raw, 1, 0, 64)
-        gout_codes, gout_scales = quantise("gout", gout_dealt)
-
-        sums = bank(0)
+        grads = [bank(4 + j) for j in range(TILES)]
         for j in range(TILES):
-            grad_bank = bank(4 + j)
-            product(grad_bank, gout_codes, gout_scales, j, val_words, val_scale[VAL_ROW:, :])
-            terms = held.tile([P, I], F32, name="terms%d" % j)
-            nc.vector.scalar_tensor_tensor(
-                blocks(terms), by_block(grad_bank), delta_col[:, j : j + 1], blocks(weighted[j]), ALU.subtract, ALU.mult
-            )
-            for b in range(BLOCKS):
-                nc.tensor.matmul(
-                    sums[:, b * P : (b + 1) * P], lhsT=terms[:, b * P : (b + 1) * P], rhs=identity[:],
-                    is_transpose=True, start=(j == 0 and b == 0), stop=(j == TILES - 1 and b == BLOCKS - 1),
+            cols = slice(j * P, (j + 1) * P)
+            product(grads[j], gout_codes[:, cols], gout_scales[:, cols], val_words, val_scale[VAL_ROW:, :])
+        out_rows = out.rearrange("(p b) g -> p b g", b=BLOCKS)
+        for side in range(2):
+            pair = slice(2 * side, 2 * side + 2)
+            sums = bank(side)
+            for j in range(TILES):
+                terms = held.tile([P, 2, P], F32, name="terms%d_%d" % (side, j))
+                nc.vector.scalar_tensor_tensor(
+                    terms[:], by_block(grads[j])[:, pair, :], delta_col[:, j : j + 1], blocks(weighted[j])[:, pair, :],
+                    ALU.subtract, ALU.mult,
                 )
-        pair_sums = held.tile([P, BLOCKS * G], F32, name="pair_sums")
-        nc.vector.tensor_reduce(pair_sums[:], sums[:].rearrange("p (c r) -> p c r", r=2), mybir.AxisListType.X, ALU.add)
-        result = held.tile([P, BLOCKS * G], F32, name="result")
-        nc.vector.tensor_tensor(result[:], pair_sums[:], old_rows[:], ALU.add)
-        nc.sync.dma_start(out.rearrange("(p b) g -> p (b g)", b=BLOCKS), result[:])
+                for b in range(2):
+                    nc.tensor.matmul(
+                        sums[:, b * P : (b + 1) * P], lhsT=terms[:, b, :], rhs=identity[:],
+                        is_transpose=True, start=(j == 0 and b == 0), stop=(j == TILES - 1 and b == 1),
+                    )
+            pair_sums = held.tile([P, 2 * G], F32, name="pair_sums%d" % side)
+            nc.vector.tensor_reduce(
+                pair_sums[:], sums[:, : 2 * P].rearrange("p (c r) -> p c r", r=2), mybir.AxisListType.X, ALU.add
+            )
+            result = held.tile([P, 2 * G], F32, name="result%d" % side)
+            nc.vector.tensor_tensor(result[:], pair_sums[:], old_rows[:, 2 * G * side : 2 * G * (side + 1)], ALU.add)
+            nc.sync.dma_start(out_rows[:, pair, :].rearrange("p b g -> p (b g)"), result[:])

@@ -20,20 +20,24 @@ PACK = 4
 TILES = Q // P
 BLOCKS = I // P
 HALF = Q // 2
-VAL_ROW = 4
-QUERY_AT = 0
-VAL_BYTES_AT = QUERY_AT + 4 * PACK * Q
-MINUS_AT = VAL_BYTES_AT + T
-KEY_SCALE_AT = MINUS_AT + 64
-WORDS_AT = KEY_SCALE_AT + I
-ZEROS_AT = VAL_BYTES_AT - 32
-ZEROS_WORDS = (WORDS_AT + 32 - ZEROS_AT) // 4
-VAL_POOL_AT = WORDS_AT + 4 * I
+ROWS = D // 32
+RAW_BYTES = 4 * PACK * HALF
+ZEROS_AT = 0
+KEY_POOL_AT = ZEROS_AT + 4 * P
+SHARP_AT = KEY_POOL_AT + 4 * T
+QUERY1_AT = SHARP_AT + 32
+LSE_AT = QUERY1_AT + RAW_BYTES
+GOUT_AT = LSE_AT + 32
+VAL_POOL_AT = GOUT_AT + 2 * RAW_BYTES
 DELTA_AT = VAL_POOL_AT + 4 * T
-OLD_AT = DELTA_AT + 32
-GOUT_AT = OLD_AT + 4 * BLOCKS * G
-LSE_AT = DELTA_AT - 32
-LSE_WORDS = (GOUT_AT + 32 - LSE_AT) // 4
+OLD_AT = DELTA_AT + 64
+VAL_PLANE_AT = OLD_AT + 4 * BLOCKS * G
+ZEROS_WORDS = (VAL_PLANE_AT + 32 - ZEROS_AT) // 4
+KEY_BYTES_AT = VAL_PLANE_AT + I
+VAL_BYTES_AT = KEY_BYTES_AT + T
+WORDS_AT = KEY_BYTES_AT + T // 2
+VAL_FIRST = 64
+SCALAR_SHARE = 18
 
 
 def tile_attend_gsharpness_kernel(
@@ -51,32 +55,27 @@ def tile_attend_gsharpness_kernel(
         def bank(n):
             return psum.tile([P, BLOCKS * P], F32, name="bank%d" % n, tag="bank%d" % n)
 
-        def load_scales(pool_bytes, scales, row):
-            for quad in range(4):
-                nc.sync.dma_start(
-                    pool_bytes[32 * quad + row : 32 * quad + row + 4, :].bitcast(I32),
-                    scales[0, 4 * quad : 4 * quad + 4, :].bitcast(I32),
-                )
-
         def words_in_hbm(words):
             return words[0].rearrange("p t r -> p (t r)").bitcast(I32)
 
-        def load_rows(raw, rows):
-            for half in range(2):
-                nc.sync.dma_start(
-                    raw[:, half, :, :], rows.rearrange("(p t) c -> p t c", t=PACK)[:, :, half * HALF : (half + 1) * HALF]
-                )
+        def load_rows(raw, rows, half):
+            nc.sync.dma_start(raw[:], rows.rearrange("(p t) c -> p t c", t=PACK)[:, :, half * HALF : (half + 1) * HALF])
 
-        lse_col = staged.tile([P, LSE_WORDS], F32, name="lse_col", offset=LSE_AT)
-        nc.sync.dma_start(lse_col[:, :TILES], lse.rearrange("o (m j) -> m (o j)", j=TILES))
-        sharp_col = held.tile([P, BLOCKS], F32, name="sharp_col")
-        nc.sync.dma_start(sharp_col[:], sharp.rearrange("(p b) o -> p (b o)", b=BLOCKS))
-        key_pool = held.tile([P, T], I32, name="key_pool")
-        nc.sync.dma_start(key_pool[:], words_in_hbm(keys_words))
+        def raw_tile(pool, name, **place):
+            return pool.tile([P, PACK, HALF], F32, name=name, **place)
 
-        key_bytes = held.tile([P, T], U8, name="key_bytes")
-        nc.gpsimd.memset(key_bytes[:].bitcast(I32), 0)
-        load_scales(key_bytes, keys_scales, 0)
+        query_raw0 = raw_tile(held, "query_raw0")
+        load_rows(query_raw0, query, 0)
+
+        key_bytes = staged.tile([P, T], U8, name="key_bytes", offset=KEY_BYTES_AT)
+        nc.vector.memset(key_bytes[:].bitcast(I32), 0)
+        for quad in range(4):
+            nc.sync.dma_start(
+                key_bytes[32 * quad : 32 * quad + 4, :].bitcast(I32), keys_scales[0, 4 * quad : 4 * quad + 4, :].bitcast(I32)
+            )
+        val_bytes = staged.tile([P, T], U8, name="val_bytes", offset=VAL_BYTES_AT)
+        nc.gpsimd.memset(val_bytes[:].bitcast(I32), 0)
+        nc.sync.dma_start(val_bytes[VAL_FIRST : VAL_FIRST + ROWS, :].bitcast(I32), vals_scales[0].bitcast(I32))
 
         zeros = staged.tile([P, ZEROS_WORDS], F32, name="zeros", offset=ZEROS_AT)
         nc.gpsimd.memset(zeros[:, :P], 0.0)
@@ -84,20 +83,21 @@ def tile_attend_gsharpness_kernel(
         nc.gpsimd.affine_select(
             out=identity[:], in_=zeros[:, :P], compare_op=ALU.not_equal, fill=1.0, base=0, pattern=[[-1, P]], channel_multiplier=1
         )
-        query_raw = staged.tile([P, 2, PACK, HALF], F32, name="query_raw", offset=QUERY_AT)
-        load_rows(query_raw, query)
+        val_plane = staged.tile([P, I], U8, name="val_plane", offset=VAL_PLANE_AT, align_bytes=64)
+        nc.gpsimd.memset(val_plane[:].bitcast(I32), 0)
 
-        val_bytes = staged.tile([P, T], U8, name="val_bytes", offset=VAL_BYTES_AT)
-        nc.vector.memset(val_bytes[:].bitcast(I32), 0)
-        load_scales(val_bytes, vals_scales, VAL_ROW)
-
-        minus_one = staged.tile([P, 1], F32, name="minus_one", offset=MINUS_AT)
-        nc.vector.memset(minus_one[:], -1.0)
-        neg_lse = held.tile([P, TILES], F32, name="neg_lse")
-        nc.scalar.activation(neg_lse[:], lse_col[:, :TILES], ACT.Copy, scale=minus_one[:])
-
-        gout_raw = staged.tile([P, 2, PACK, HALF], F32, name="gout_raw", offset=GOUT_AT)
-        load_rows(gout_raw, gout)
+        key_pool = staged.tile([P, T], I32, name="key_pool", offset=KEY_POOL_AT)
+        nc.sync.dma_start(key_pool[:], words_in_hbm(keys_words))
+        sharp_col = staged.tile([P, BLOCKS], F32, name="sharp_col", offset=SHARP_AT)
+        nc.sync.dma_start(sharp_col[:], sharp.rearrange("(p b) o -> p (b o)", b=BLOCKS))
+        query_raw1 = raw_tile(staged, "query_raw1", offset=QUERY1_AT)
+        load_rows(query_raw1, query, 1)
+        lse_col = staged.tile([P, TILES], F32, name="lse_col", offset=LSE_AT)
+        nc.sync.dma_start(lse_col[:], lse.rearrange("o (m j) -> m (o j)", j=TILES))
+        gout_raw0 = raw_tile(staged, "gout_raw0", offset=GOUT_AT)
+        load_rows(gout_raw0, gout, 0)
+        gout_raw1 = raw_tile(staged, "gout_raw1", offset=GOUT_AT + RAW_BYTES)
+        load_rows(gout_raw1, gout, 1)
         val_pool = staged.tile([P, T], I32, name="val_pool", offset=VAL_POOL_AT)
         nc.sync.dma_start(val_pool[:], words_in_hbm(vals_words))
         delta_col = staged.tile([P, TILES], F32, name="delta_col", offset=DELTA_AT)
@@ -105,22 +105,28 @@ def tile_attend_gsharpness_kernel(
         old_rows = staged.tile([P, BLOCKS * G], F32, name="old_rows", offset=OLD_AT)
         nc.sync.dma_start(old_rows[:], old.rearrange("(p b) g -> p (b g)", b=BLOCKS))
 
-        sharp_bank = bank(4)
-        for b in range(BLOCKS):
-            nc.tensor.transpose(
-                sharp_bank[:, b * P : (b + 1) * P], sharp_col[:, b : b + 1].to_broadcast([P, P]), identity[:]
-            )
-        sharp_row = held.tile([P, I], F32, name="sharp_row", tag="sharp_row", align_bytes=64)
-        nc.scalar.copy(sharp_row[:], sharp_bank[:])
 
         def gather(picked, window):
             nc.vector.tensor_copy(picked[:], window.indirect(offsets[:]))
+
+        key_plane = held.tile([P, I], U8, name="key_plane", align_bytes=64)
+        gather(key_plane, key_bytes[:])
+        val_scale = held.tile([P, I], U8, name="val_scale")
+        gather(val_scale, val_bytes[:])
+        for quad in range(4):
+            first = VAL_FIRST + 4 * quad
+            nc.sync.dma_start(
+                val_plane[32 * quad : 32 * quad + 4, :].bitcast(I32), val_scale[first : first + 4, :].bitcast(I32)
+            )
+
+        def scalar_cast(dst, src):
+            nc.scalar.activation(dst, src, ACT.Copy)
 
         def round_and_deal(copy, dealt, raw, half, m0, m1):
             base = half * (P // 2)
             copy(
                 dealt[:, :, base + m0 : base + m1, :].rearrange("p j m t -> p m t j"),
-                raw[:, half, :, m0 * TILES : m1 * TILES].rearrange("p t (m j) -> p m t j", j=TILES),
+                raw[:, :, m0 * TILES : m1 * TILES].rearrange("p t (m j) -> p m t j", j=TILES),
             )
 
         def quantise(codes, scales, dealt):
@@ -140,66 +146,71 @@ def tile_attend_gsharpness_kernel(
 
         key_words = staged.tile([P, I], U32, name="key_words", offset=WORDS_AT, align_bytes=64)
         gather(key_words, key_pool[:].bitcast(U32))
-        key_scale = staged.tile([P, I], U8, name="key_scale", offset=KEY_SCALE_AT, align_bytes=64)
-        gather(key_scale, key_bytes[:])
 
-        query_dealt = held.tile([P, TILES, P, PACK], BF16, name="query_dealt", tag="query_dealt", align_bytes=64)
-        round_and_deal(nc.scalar.copy, query_dealt, query_raw, 0, 0, 64)
-        round_and_deal(nc.scalar.copy, query_dealt, query_raw, 1, 0, 18)
-        round_and_deal(nc.vector.tensor_copy, query_dealt, query_raw, 1, 18, 64)
+        query_dealt = held.tile([P, TILES, P, PACK], BF16, name="query_dealt", align_bytes=64)
+        round_and_deal(scalar_cast, query_dealt, query_raw0, 0, 0, 64)
+        sharp_bank = bank(4)
+        for b in range(BLOCKS):
+            nc.tensor.transpose(
+                sharp_bank[:, b * P : (b + 1) * P], sharp_col[:, b : b + 1].to_broadcast([P, P]), identity[:]
+            )
+        sharp_row = held.tile([P, I], F32, name="sharp_row", tag="sharp_row", align_bytes=64)
+        nc.scalar.copy(sharp_row[:], sharp_bank[:])
+
+        round_and_deal(scalar_cast, query_dealt, query_raw1, 1, 0, SCALAR_SHARE)
+        round_and_deal(nc.vector.tensor_copy, query_dealt, query_raw1, 1, SCALAR_SHARE, 64)
         query_codes = [held.tile([P, P], U32, name="query_codes%d" % j, align_bytes=64) for j in range(TILES)]
         query_scales = [held.tile([P, P], U8, name="query_scales%d" % j, align_bytes=64) for j in range(TILES)]
         for j in range(TILES):
             quantise(query_codes[j][:], query_scales[j][:], query_dealt[:, j : j + 1, :, :])
+        neg_lse = held.tile([P, TILES], F32, name="neg_lse")
+        nc.scalar.activation(neg_lse[:], lse_col[:], ACT.Copy, scale=-1.0)
         gout_dealt = held.tile([P, TILES, P, PACK], BF16, name="gout_dealt", align_bytes=64)
-        round_and_deal(nc.scalar.copy, gout_dealt, gout_raw, 0, 0, 64)
-        round_and_deal(nc.scalar.copy, gout_dealt, gout_raw, 1, 0, 64)
-        val_scale = held.tile([P, I], U8, name="val_scale", tag="query_dealt", align_bytes=64)
-        gather(val_scale, val_bytes[:])
+        round_and_deal(scalar_cast, gout_dealt, gout_raw0, 0, 0, 64)
+        round_and_deal(scalar_cast, gout_dealt, gout_raw1, 1, 0, 64)
 
         scores = [bank(j) for j in range(TILES)]
         weighted = []
-        exps = []
+        weights = staged.tile([P, TILES, I], F32, name="weights", offset=GOUT_AT)
         for j in range(TILES):
-            product(scores[j], query_codes[j][:], query_scales[j][:], key_words, key_scale[:])
+            product(scores[j], query_codes[j][:], query_scales[j][:], key_words, key_plane[:])
             logits = held.tile([P, I], F32, name="logits%d" % j)
             nc.vector.tensor_tensor(blocks(logits), by_block(scores[j]), blocks(sharp_row), ALU.mult)
-            weights = staged.tile([P, I], F32, name="weights%d" % j, offset=GOUT_AT + 4 * I * j)
-            nc.scalar.activation(weights[:], logits[:], ACT.Exp, bias=neg_lse[:, j : j + 1], scale=1.0)
-            exps.append(weights)
+            nc.scalar.activation(weights[:, j, :], logits[:], ACT.Exp, bias=neg_lse[:, j : j + 1], scale=1.0)
         gout_codes = held.tile([P, Q], U32, name="gout_codes", tag="sharp_row", align_bytes=64)
         gout_scales = held.tile([P, Q], U8, name="gout_scales", align_bytes=64)
         quantise(gout_codes[:], gout_scales[:], gout_dealt[:])
-        val_words = staged.tile([P, I], U32, name="val_words2", offset=WORDS_AT, align_bytes=64)
+        val_words = staged.tile([P, I], U32, name="val_words", offset=WORDS_AT, align_bytes=64)
         gather(val_words, val_pool[:].bitcast(U32))
         for j in range(TILES):
             both = staged.tile([P, I], F32, name="weighted%d" % j, offset=VAL_POOL_AT + 4 * I * j)
-            nc.vector.scalar_tensor_tensor(blocks(both), by_block(scores[j]), 512.0, blocks(exps[j]), ALU.mult, ALU.mult)
+            nc.vector.scalar_tensor_tensor(blocks(both), by_block(scores[j]), 512.0, weights[:, j, :].rearrange("m (b p) -> m b p", b=BLOCKS), ALU.mult, ALU.mult)
             weighted.append(both)
 
         grads = [bank(4 + j) for j in range(TILES)]
         for j in range(TILES):
             cols = slice(j * P, (j + 1) * P)
-            product(grads[j], gout_codes[:, cols], gout_scales[:, cols], val_words, val_scale[VAL_ROW:, :])
-        out_rows = out.rearrange("(p b) g -> p b g", b=BLOCKS)
-        for side in range(2):
-            pair = slice(2 * side, 2 * side + 2)
-            sums = bank(side)
-            for j in range(TILES):
-                terms = held.tile([P, 2, P], F32, name="terms%d_%d" % (side, j))
+            product(grads[j], gout_codes[:, cols], gout_scales[:, cols], val_words, val_plane[:])
+        sums = [bank(side) for side in range(2)]
+        for j in range(TILES):
+            last = j == TILES - 1
+            terms = held.tile([P, BLOCKS, P], F32, name="terms%d" % j)
+            for part in [slice(0, 2), slice(2, 4)] if last else [slice(0, 4)]:
                 nc.vector.scalar_tensor_tensor(
-                    terms[:], by_block(grads[j])[:, pair, :], delta_col[:, j : j + 1], blocks(weighted[j])[:, pair, :],
-                    ALU.subtract, ALU.mult,
+                    terms[:, part, :], by_block(grads[j])[:, part, :], delta_col[:, j : j + 1],
+                    blocks(weighted[j])[:, part, :], ALU.subtract, ALU.mult,
                 )
-                for b in range(2):
+                for b in range(part.start, part.stop):
                     nc.tensor.matmul(
-                        sums[:, b * P : (b + 1) * P], lhsT=terms[:, b, :], rhs=identity[:],
-                        is_transpose=True, start=(j == 0 and b == 0), stop=(j == TILES - 1 and b == 1),
+                        sums[b // 2][:, (b % 2) * P : (b % 2 + 1) * P], lhsT=terms[:, b, :], rhs=identity[:],
+                        is_transpose=True, start=(j == 0 and b % 2 == 0), stop=(last and b % 2 == 1),
                     )
-            pair_sums = held.tile([P, 2 * G], F32, name="pair_sums%d" % side)
-            nc.vector.tensor_reduce(
-                pair_sums[:], sums[:, : 2 * P].rearrange("p (c r) -> p c r", r=2), mybir.AxisListType.X, ALU.add
-            )
+        out_rows = out.rearrange("(p b) g -> p (b g)", b=BLOCKS)
+        for side in range(2):
+            cols = slice(2 * G * side, 2 * G * (side + 1))
+            halves = sums[side][:, : 2 * P].rearrange("p (c r) -> p r c", r=2)
+            partial = held.tile([P, 2 * G], F32, name="partial%d" % side)
+            nc.vector.tensor_tensor(partial[:], halves[:, 0, :], old_rows[:, cols], ALU.add)
             result = held.tile([P, 2 * G], F32, name="result%d" % side)
-            nc.vector.tensor_tensor(result[:], pair_sums[:], old_rows[:, 2 * G * side : 2 * G * (side + 1)], ALU.add)
-            nc.sync.dma_start(out_rows[:, pair, :].rearrange("p b g -> p (b g)"), result[:])
+            nc.vector.tensor_tensor(result[:], halves[:, 1, :], partial[:], ALU.add)
+            nc.sync.dma_start(out_rows[:, cols], result[:])

@@ -38,6 +38,7 @@ VAL_BYTES_AT = KEY_BYTES_AT + T
 WORDS_AT = KEY_BYTES_AT + T // 2
 VAL_FIRST = 64
 SCALAR_SHARE = 18
+VECTOR_TILES = 2
 
 
 def tile_attend_gsharpness_kernel(
@@ -165,7 +166,7 @@ def tile_attend_gsharpness_kernel(
             quantise(query_codes[j][:], query_scales[j][:], query_dealt[:, j : j + 1, :, :])
         neg_lse = held.tile([P, TILES], F32, name="neg_lse")
         nc.scalar.activation(neg_lse[:], lse_col[:], ACT.Copy, scale=-1.0)
-        gout_dealt = held.tile([P, TILES, P, PACK], BF16, name="gout_dealt", align_bytes=64)
+        gout_dealt = held.tile([P, TILES, P, PACK], BF16, name="gout_dealt", tag="gout_dealt", align_bytes=64)
         round_and_deal(scalar_cast, gout_dealt, gout_raw0, 0, 0, 64)
         round_and_deal(scalar_cast, gout_dealt, gout_raw1, 1, 0, 64)
 
@@ -174,17 +175,22 @@ def tile_attend_gsharpness_kernel(
         weights = staged.tile([P, TILES, I], F32, name="weights", offset=GOUT_AT)
         for j in range(TILES):
             product(scores[j], query_codes[j][:], query_scales[j][:], key_words, key_plane[:])
-            logits = held.tile([P, I], F32, name="logits%d" % j)
+            logits = held.tile([P, I], F32, name="logits%d" % j, tag="logits%d" % j)
             nc.vector.tensor_tensor(blocks(logits), by_block(scores[j]), blocks(sharp_row), ALU.mult)
             nc.scalar.activation(weights[:, j, :], logits[:], ACT.Exp, bias=neg_lse[:, j : j + 1], scale=1.0)
         gout_codes = held.tile([P, Q], U32, name="gout_codes", tag="sharp_row", align_bytes=64)
         gout_scales = held.tile([P, Q], U8, name="gout_scales", align_bytes=64)
         quantise(gout_codes[:], gout_scales[:], gout_dealt[:])
-        val_words = staged.tile([P, I], U32, name="val_words", offset=WORDS_AT, align_bytes=64)
+        val_words = held.tile([P, I], U32, name="val_words", tag="gout_dealt", align_bytes=64)
         gather(val_words, val_pool[:].bitcast(U32))
         for j in range(TILES):
             both = staged.tile([P, I], F32, name="weighted%d" % j, offset=VAL_POOL_AT + 4 * I * j)
-            nc.vector.scalar_tensor_tensor(blocks(both), by_block(scores[j]), 512.0, weights[:, j, :].rearrange("m (b p) -> m b p", b=BLOCKS), ALU.mult, ALU.mult)
+            if j < VECTOR_TILES:
+                nc.vector.scalar_tensor_tensor(blocks(both), by_block(scores[j]), 512.0, weights[:, j, :].rearrange("m (b p) -> m b p", b=BLOCKS), ALU.mult, ALU.mult)
+            else:
+                scaled = held.tile([P, I], F32, name="scaled%d" % j, tag="logits%d" % j)
+                nc.scalar.activation(blocks(scaled), by_block(scores[j]), ACT.Copy, scale=512.0)
+                nc.gpsimd.tensor_tensor(both[:], scaled[:], weights[:, j, :], ALU.mult)
             weighted.append(both)
 
         grads = [bank(4 + j) for j in range(TILES)]

from contextlib import ExitStack

import concourse.mybir as mybir

D, E, T, I, Q, G = 512, 512, 2048, 512, 512, 64
FLOPS = 2 * I * Q * (D + E)

F32 = mybir.dt.float32
BF16 = mybir.dt.bfloat16
I32 = mybir.dt.int32
U32 = mybir.dt.uint32
U16 = mybir.dt.uint16
U8 = mybir.dt.uint8
FP8X4 = mybir.dt.float8_e4m3fn_x4
ALU = mybir.AluOpType
ACT = mybir.ActivationFunctionType

P = 128
PACK = 4
TILES = Q // P
BLOCKS = I // P
HALF = Q // 2
ROWS = D // 32
RAW_BYTES = 4 * PACK * HALF
ZEROS_AT = 0
KEY_POOL_AT = ZEROS_AT + 4 * P
SHARP_AT = KEY_POOL_AT + 4 * T
QUERY1_AT = SHARP_AT + 32
LSE_AT = QUERY1_AT + RAW_BYTES
GOUT_AT = LSE_AT + 32
VAL_POOL_AT = GOUT_AT + 2 * RAW_BYTES
DELTA_AT = VAL_POOL_AT + 4 * T
OLD_AT = DELTA_AT + 64
VAL_PLANE_AT = OLD_AT + 4 * BLOCKS * G
ZEROS_WORDS = (VAL_PLANE_AT + 32 - ZEROS_AT) // 4
KEY_BYTES_AT = VAL_PLANE_AT + I
VAL_BYTES_AT = KEY_BYTES_AT + T
WORDS_AT = KEY_BYTES_AT + T // 2
VAL_FIRST = 64
SCALAR_SHARE = 18
VECTOR_TILES = 2


def tile_attend_gsharpness_kernel(
    tc, query, keys_words, keys_scales, sharp, lse, gout, vals_words, vals_scales, delta, old, offs, out
):
    nc = tc.nc
    with ExitStack() as ctx:
        held = ctx.enter_context(tc.tile_pool(name="held", bufs=1))
        staged = ctx.enter_context(tc.tile_pool(name="staged", bufs=1))
        psum = ctx.enter_context(tc.psum_pool(name="psum", bufs=1))

        offsets = held.tile([P, I // 16], U16, name="offsets")
        nc.sync.dma_start(offsets[:], offs)

        def bank(n):
            return psum.tile([P, BLOCKS * P], F32, name="bank%d" % n, tag="bank%d" % n)

        def words_in_hbm(words):
            return words[0].rearrange("p t r -> p (t r)").bitcast(I32)

        def load_rows(raw, rows, half):
            nc.sync.dma_start(raw[:], rows.rearrange("(p t) c -> p t c", t=PACK)[:, :, half * HALF : (half + 1) * HALF])

        def raw_tile(pool, name, **place):
            return pool.tile([P, PACK, HALF], F32, name=name, **place)

        query_raw0 = raw_tile(held, "query_raw0")
        load_rows(query_raw0, query, 0)

        key_bytes = staged.tile([P, T], U8, name="key_bytes", offset=KEY_BYTES_AT)
        nc.vector.memset(key_bytes[:].bitcast(I32), 0)
        for quad in range(4):
            nc.sync.dma_start(
                key_bytes[32 * quad : 32 * quad + 4, :].bitcast(I32), keys_scales[0, 4 * quad : 4 * quad + 4, :].bitcast(I32)
            )
        val_bytes = staged.tile([P, T], U8, name="val_bytes", offset=VAL_BYTES_AT)
        nc.gpsimd.memset(val_bytes[:].bitcast(I32), 0)
        nc.sync.dma_start(val_bytes[VAL_FIRST : VAL_FIRST + ROWS, :].bitcast(I32), vals_scales[0].bitcast(I32))

        zeros = staged.tile([P, ZEROS_WORDS], F32, name="zeros", offset=ZEROS_AT)
        nc.gpsimd.memset(zeros[:, :P], 0.0)
        identity = held.tile([P, P], F32, name="identity")
        nc.gpsimd.affine_select(
            out=identity[:], in_=zeros[:, :P], compare_op=ALU.not_equal, fill=1.0, base=0, pattern=[[-1, P]], channel_multiplier=1
        )
        val_plane = staged.tile([P, I], U8, name="val_plane", offset=VAL_PLANE_AT, align_bytes=64)
        nc.gpsimd.memset(val_plane[:].bitcast(I32), 0)

        key_pool = staged.tile([P, T], I32, name="key_pool", offset=KEY_POOL_AT)
        nc.sync.dma_start(key_pool[:], words_in_hbm(keys_words))
        sharp_col = staged.tile([P, BLOCKS], F32, name="sharp_col", offset=SHARP_AT)
        nc.sync.dma_start(sharp_col[:], sharp.rearrange("(p b) o -> p (b o)", b=BLOCKS))
        query_raw1 = raw_tile(staged, "query_raw1", offset=QUERY1_AT)
        load_rows(query_raw1, query, 1)
        lse_col = staged.tile([P, TILES], F32, name="lse_col", offset=LSE_AT)
        nc.sync.dma_start(lse_col[:], lse.rearrange("o (m j) -> m (o j)", j=TILES))
        gout_raw0 = raw_tile(staged, "gout_raw0", offset=GOUT_AT)
        load_rows(gout_raw0, gout, 0)
        gout_raw1 = raw_tile(staged, "gout_raw1", offset=GOUT_AT + RAW_BYTES)
        load_rows(gout_raw1, gout, 1)
        val_pool = staged.tile([P, T], I32, name="val_pool", offset=VAL_POOL_AT)
        nc.sync.dma_start(val_pool[:], words_in_hbm(vals_words))
        delta_col = staged.tile([P, TILES], F32, name="delta_col", offset=DELTA_AT)
        nc.sync.dma_start(delta_col[:], delta.rearrange("o (m j) -> m (o j)", j=TILES))
        old_rows = staged.tile([P, BLOCKS * G], F32, name="old_rows", offset=OLD_AT)
        nc.sync.dma_start(old_rows[:], old.rearrange("(p b) g -> p (b g)", b=BLOCKS))


        def gather(picked, window):
            nc.vector.tensor_copy(picked[:], window.indirect(offsets[:]))

        key_plane = held.tile([P, I], U8, name="key_plane", align_bytes=64)
        gather(key_plane, key_bytes[:])
        val_scale = held.tile([P, I], U8, name="val_scale")
        gather(val_scale, val_bytes[:])
        for quad in range(4):
            first = VAL_FIRST + 4 * quad
            nc.sync.dma_start(
                val_plane[32 * quad : 32 * quad + 4, :].bitcast(I32), val_scale[first : first + 4, :].bitcast(I32)
            )

        def scalar_cast(dst, src):
            nc.scalar.activation(dst, src, ACT.Copy)

        def round_and_deal(copy, dealt, raw, half, m0, m1):
            base = half * (P // 2)
            copy(
                dealt[:, :, base + m0 : base + m1, :].rearrange("p j m t -> p m t j"),
                raw[:, :, m0 * TILES : m1 * TILES].rearrange("p t (m j) -> p m t j", j=TILES),
            )

        def quantise(codes, scales, dealt):
            nc.vector.quantize_mx(codes.bitcast(FP8X4), scales, dealt.rearrange("p j m t -> p (j m t)"))

        def product(acc, codes, scales, words, word_scales):
            nc.tensor.matmul_mx(
                acc[:], lhsT=codes.bitcast(FP8X4), lhsT_scale=scales,
                rhs=words[:].bitcast(FP8X4), rhs_scale=word_scales, start=True, stop=True,
            )

        def by_block(acc):
            return acc[:].rearrange("m (p b) -> m b p", b=BLOCKS)

        def blocks(tile):
            return tile[:].rearrange("m (b p) -> m b p", b=BLOCKS)

        key_words = staged.tile([P, I], U32, name="key_words", offset=WORDS_AT, align_bytes=64)
        gather(key_words, key_pool[:].bitcast(U32))

        query_dealt = held.tile([P, TILES, P, PACK], BF16, name="query_dealt", align_bytes=64)
        round_and_deal(scalar_cast, query_dealt, query_raw0, 0, 0, 64)
        sharp_bank = bank(4)
        for b in range(BLOCKS):
            nc.tensor.transpose(
                sharp_bank[:, b * P : (b + 1) * P], sharp_col[:, b : b + 1].to_broadcast([P, P]), identity[:]
            )
        sharp_row = held.tile([P, I], F32, name="sharp_row", tag="sharp_row", align_bytes=64)
        nc.scalar.copy(sharp_row[:], sharp_bank[:])

        round_and_deal(scalar_cast, query_dealt, query_raw1, 1, 0, SCALAR_SHARE)
        round_and_deal(nc.vector.tensor_copy, query_dealt, query_raw1, 1, SCALAR_SHARE, 64)
        query_codes = [held.tile([P, P], U32, name="query_codes%d" % j, align_bytes=64) for j in range(TILES)]
        query_scales = [held.tile([P, P], U8, name="query_scales%d" % j, align_bytes=64) for j in range(TILES)]
        for j in range(TILES):
            quantise(query_codes[j][:], query_scales[j][:], query_dealt[:, j : j + 1, :, :])
        neg_lse = held.tile([P, TILES], F32, name="neg_lse")
        nc.scalar.activation(neg_lse[:], lse_col[:], ACT.Copy, scale=-1.0)
        gout_dealt = held.tile([P, TILES, P, PACK], BF16, name="gout_dealt", tag="gout_dealt", align_bytes=64)
        round_and_deal(scalar_cast, gout_dealt, gout_raw0, 0, 0, 64)
        round_and_deal(scalar_cast, gout_dealt, gout_raw1, 1, 0, 64)

        scores = [bank(j) for j in range(TILES)]
        weighted = []
        weights = staged.tile([P, TILES, I], F32, name="weights", offset=GOUT_AT)
        for j in range(TILES):
            product(scores[j], query_codes[j][:], query_scales[j][:], key_words, key_plane[:])
            logits = held.tile([P, I], F32, name="logits%d" % j, tag="logits%d" % j)
            nc.vector.tensor_tensor(blocks(logits), by_block(scores[j]), blocks(sharp_row), ALU.mult)
            nc.scalar.activation(weights[:, j, :], logits[:], ACT.Exp, bias=neg_lse[:, j : j + 1], scale=1.0)
        gout_codes = held.tile([P, Q], U32, name="gout_codes", tag="sharp_row", align_bytes=64)
        gout_scales = held.tile([P, Q], U8, name="gout_scales", align_bytes=64)
        quantise(gout_codes[:], gout_scales[:], gout_dealt[:])
        val_words = held.tile([P, I], U32, name="val_words", tag="gout_dealt", align_bytes=64)
        gather(val_words, val_pool[:].bitcast(U32))
        for j in range(TILES):
            both = staged.tile([P, I], F32, name="weighted%d" % j, offset=VAL_POOL_AT + 4 * I * j)
            if j < VECTOR_TILES:
                nc.vector.scalar_tensor_tensor(blocks(both), by_block(scores[j]), 512.0, weights[:, j, :].rearrange("m (b p) -> m b p", b=BLOCKS), ALU.mult, ALU.mult)
            else:
                scaled = held.tile([P, I], F32, name="scaled%d" % j, tag="logits%d" % j)
                nc.scalar.activation(blocks(scaled), by_block(scores[j]), ACT.Copy, scale=512.0)
                nc.gpsimd.tensor_tensor(both[:], scaled[:], weights[:, j, :], ALU.mult)
            weighted.append(both)

        grads = [bank(4 + j) for j in range(TILES)]
        for j in range(TILES):
            cols = slice(j * P, (j + 1) * P)
            product(grads[j], gout_codes[:, cols], gout_scales[:, cols], val_words, val_plane[:])
        sums = [bank(side) for side in range(2)]
        for j in range(TILES):
            last = j == TILES - 1
            terms = held.tile([P, BLOCKS, P], F32, name="terms%d" % j)
            for part in [slice(0, 2), slice(2, 4)] if last else [slice(0, 4)]:
                nc.vector.scalar_tensor_tensor(
                    terms[:, part, :], by_block(grads[j])[:, part, :], delta_col[:, j : j + 1],
                    blocks(weighted[j])[:, part, :], ALU.subtract, ALU.mult,
                )
                for b in range(part.start, part.stop):
                    nc.tensor.matmul(
                        sums[b // 2][:, (b % 2) * P : (b % 2 + 1) * P], lhsT=terms[:, b, :], rhs=identity[:],
                        is_transpose=True, start=(j == 0 and b % 2 == 0), stop=(last and b % 2 == 1),
                    )
        out_rows = out.rearrange("(p b) g -> p (b g)", b=BLOCKS)
        for side in range(2):
            cols = slice(2 * G * side, 2 * G * (side + 1))
            halves = sums[side][:, : 2 * P].rearrange("p (c r) -> p r c", r=2)
            partial = held.tile([P, 2 * G], F32, name="partial%d" % side)
            nc.vector.tensor_tensor(partial[:], halves[:, 0, :], old_rows[:, cols], ALU.add)
            result = held.tile([P, 2 * G], F32, name="result%d" % side)
            nc.vector.tensor_tensor(result[:], halves[:, 1, :], partial[:], ALU.add)
            nc.sync.dma_start(out_rows[:, cols], result[:])
